import numpy as np
import ml_dtypes


def mxq(x, axis, fmt="e4m3"):
    dtype, down = {"e4m3": (ml_dtypes.float8_e4m3fn, 7), "e5m2": (ml_dtypes.float8_e5m2, 14)}[fmt]
    v = np.moveaxis(np.asarray(x, np.float32).astype(ml_dtypes.bfloat16).astype(np.float64), axis, -1)
    blocks = v.reshape(v.shape[:-1] + (-1, 32))
    amax = np.abs(blocks).max(-1, keepdims=True)
    byte = np.maximum(np.where(amax > 0, np.frexp(amax)[1] - 1 + 127, 0) - down, 1)
    scale = np.exp2(byte - 127.0)
    codes = (blocks / scale).astype(np.float32).astype(dtype).astype(np.float64)
    return np.moveaxis((codes * scale).reshape(v.shape), -1, axis)


WIDE = False


def mx_kscale(k):
    if not WIDE:
        return np.ones(k)
    levels = np.array([10, -10, 5, -5, 0])
    if k % 512:
        return np.exp2(np.random.permutation(np.resize(levels, k // 32))).repeat(32)
    a = np.empty((k // 512, 16))
    for p in range(k // 512):
        a[p, :8] = np.random.permutation(np.resize(levels, 8))
        for g in range(8):
            far = levels[np.abs(levels - a[p, g]) >= 10]
            a[p, g + 8] = far[np.random.randint(len(far))]
    return np.exp2(a.ravel()).repeat(32)


def f64(x):
    return np.asarray(x).astype(np.float64)


def striped(idx):
    return np.tile(idx.reshape(-1, 16).T, (8, 1)).astype(np.uint16)


def unstriped(offs):
    return offs[:16].T.reshape(-1).astype(np.int64)


E2M1 = np.array([0.0, 0.5, 1.0, 1.5, 2.0, 3.0, 4.0, 6.0, -0.0, -0.5, -1.0, -1.5, -2.0, -3.0, -4.0, -6.0])


def pack_fp4(w):
    k, n = w.shape
    w = f64(np.asarray(w, np.float32).astype(ml_dtypes.bfloat16)).reshape(k // 32, 32, n)
    amax = np.abs(w).max(1)
    mant, ex = np.frexp(amax / 6.0)
    byte = np.clip(np.where(amax > 0, np.where(mant > 0.5, ex, ex - 1) + 127, 1), 1, 254)
    scaled = (w * np.exp2(127.0 - byte)[:, None, :]).reshape(k, n).astype(np.float32)
    c = np.ascontiguousarray(scaled.reshape(k // 512, 128, 4, n).transpose(0, 1, 3, 2)).astype(ml_dtypes.float4_e2m1fn).view(np.uint8) & 0xF
    words = (c[..., 0::2] | (c[..., 1::2] << 4)).reshape(k // 512, 128, 2 * n)
    return np.ascontiguousarray(words), np.ascontiguousarray(byte.astype(np.uint8).reshape(k // 512, 16, n))


def unpack_fp4(words, scales):
    g, _, n = scales.shape
    words = np.ascontiguousarray(words).reshape(g, 128, n, 2)
    nib = np.empty((g, 128, n, 4), np.uint8)
    nib[..., 0::2] = words & 0xF
    nib[..., 1::2] = words >> 4
    vals = E2M1[nib] * np.repeat(np.exp2(scales.astype(np.float64) - 127.0), 8, axis=1)[..., None]
    return vals.transpose(0, 1, 3, 2).reshape(g * 512, n)


def relu(v):
    return np.maximum(v, 0.0)


def sigmoid(v):
    return 1.0 / (1.0 + np.exp(-np.maximum(v, -700.0)))


K, T, S, N, U = 512, 2048, 1024, 128, 2048


def setup_inputs():
    n = np.random.standard_normal
    s = mx_kscale(K)[:, None]
    packed_w1 = pack_fp4(n((K, N)) / np.sqrt(K) / s)
    packed_w2 = pack_fp4(n((K, N)) / np.sqrt(K) / s)
    return {
        "xT": (n((K, T)) * s).astype(np.float32),
        "mem": n((N, U)).astype(np.float32),
        "w1_words": packed_w1[0],
        "w1_scales": packed_w1[1],
        "w2_words": packed_w2[0],
        "w2_scales": packed_w2[1],
        "offs": striped(np.random.permutation(T)[:S]),
        "slot": striped(np.random.permutation(U)[:S]),
    }


def reference(xT, mem, w1_words, w1_scales, w2_words, w2_scales, offs, slot):
    old = f64(mem)[:, unstriped(slot)]
    xq = mxq(f64(xT)[:, unstriped(offs)], 0, "e4m3")
    g = sigmoid(unpack_fp4(w2_words, w2_scales).T @ xq)
    y = relu(unpack_fp4(w1_words, w1_scales).T @ xq)
    out = f64(mem).copy()
    out[:, unstriped(slot)] = old + g * (y - old)
    return out

@@ -1,0 +1,128 @@
+from contextlib import ExitStack
+
+import concourse.mybir as mybir
+
+K, T, S, N = 512, 2048, 1024, 128
+FLOPS = 2 * 2 * K * S * N
+
+F32 = mybir.dt.float32
+BF16 = mybir.dt.bfloat16
+I32 = mybir.dt.int32
+U32 = mybir.dt.uint32
+U16 = mybir.dt.uint16
+U8 = mybir.dt.uint8
+FP8X4 = mybir.dt.float8_e4m3fn_x4
+FP4X4 = mybir.dt.float4_e2m1fn_x4
+ACT = mybir.ActivationFunctionType
+ALU = mybir.AluOpType
+
+P = 128
+PAIR_COLS = [640,640,512,256]
+ROW2_COLS = [1024,1024]
+ROW3_COLS = [1024,768,256]
+CHUNKS = [512,512]
+
+
+def spans(widths):
+    return [(sum(widths[:i]), sum(widths[: i + 1])) for i in range(len(widths))]
+
+
+def tile_picked_gmem_relu_e_kernel(tc, xT, mem, w1_words, w1_scales, w2_words, w2_scales, offs, slot, out):
+    nc = tc.nc
+    x_rows = xT.rearrange("(p j) t -> p j t", j=4)
+
+    with ExitStack() as ctx:
+        keep = ctx.enter_context(tc.tile_pool(name="keep", bufs=1))
+        psum = ctx.enter_context(tc.psum_pool(name="psum", bufs=1))
+
+        offs_sb = keep.tile([P, S // 16], U16, name="offs_sb")
+        slot_sb = keep.tile([P, S // 16], U16, name="slot_sb")
+        memory = keep.tile([P, T], F32, name="memory")
+        pairs = keep.tile([P, T], U32, name="pairs")
+        row2 = keep.tile([P, T], BF16, name="row2")
+        row3 = keep.tile([P, T], BF16, name="row3")
+        old = keep.tile([P, S], F32, name="old")
+        step = keep.tile([P, S], F32, name="step")
+
+        warm_in = keep.tile([P, 1], F32, name="warm_in")
+        warm_out = keep.tile([P, 1], F32, name="warm_out")
+        nc.vector.memset(warm_in[:], 0.0)
+        nc.scalar.activation(warm_out[:], warm_in[:], ACT.Sigmoid)
+
+        words = []
+        scales = []
+        for i, w_scales in enumerate((w1_scales, w2_scales)):
+            ws = keep.tile([P, N], U8, name=f"w_scales{i}", align_bytes=64)
+            nc.vector.memset(ws[:].bitcast(I32), 0)
+            for q in range(4):
+                nc.gpsimd.dma_start(ws[32 * q : 32 * q + 4, :].bitcast(I32), w_scales[0, 4 * q : 4 * q + 4, :].bitcast(I32))
+            scales.append(ws)
+
+        for i, (a, b) in enumerate(spans(ROW2_COLS)):
+            raw = keep.tile([P, b - a], F32, name=f"raw_row2_{i}")
+            nc.sync.dma_start(raw[:], x_rows[:, 2, a:b])
+            nc.scalar.activation(row2[:, a:b], raw[:], ACT.Copy)
+        nc.sync.dma_start(offs_sb[:], offs)
+
+        pairs_bf = pairs[:].bitcast(BF16).rearrange("p (t u) -> p t u", u=2)
+        for i, (a, b) in enumerate(spans(PAIR_COLS)):
+            raw = keep.tile([P, 2, b - a], F32, name=f"raw_pair{i}")
+            nc.sync.dma_start(raw[:], x_rows[:, 0:2, a:b])
+            nc.vector.tensor_copy(pairs_bf[:, a:b, :], raw[:].rearrange("p u t -> p t u"))
+
+        picked = []
+        for c, (a, b) in enumerate(spans(CHUNKS)):
+            g = keep.tile([P, 4 * (b - a)], BF16, name=f"picked{c}", align_bytes=64)
+            picked.append(g)
+            g4 = g[:].rearrange("p (n j) -> p n j", j=4)
+            nc.scalar.activation(g4[:, :, 2], row2[:].indirect(offs_sb[:, a // 16 : b // 16]), ACT.Copy)
+        for c, (a, b) in enumerate(spans(CHUNKS)):
+            g_words = picked[c][:].bitcast(U32).rearrange("p (n u) -> p n u", u=2)
+            nc.vector.tensor_copy(g_words[:, :, 0], pairs[:].indirect(offs_sb[:, a // 16 : b // 16]))
+
+        for i, (a, b) in enumerate(spans(ROW3_COLS)):
+            raw = keep.tile([P, b - a], F32, name=f"raw_row3_{i}")
+            nc.sync.dma_start(raw[:], x_rows[:, 3, a:b])
+            nc.scalar.activation(row3[:, a:b], raw[:], ACT.Copy)
+        for i, w_words in enumerate((w1_words, w2_words)):
+            ww = keep.tile([P, 2 * N], U8, name=f"w_words{i}", align_bytes=64)
+            nc.sync.dma_start(ww[:], w_words[0])
+            words.append(ww)
+        nc.sync.dma_start(slot_sb[:], slot)
+        nc.sync.dma_start(memory[:], mem)
+
+        gates = []
+        cands = []
+        for c, (a, b) in enumerate(spans(CHUNKS)):
+            n = b - a
+            cols = slice(a // 16, b // 16)
+            g4 = picked[c][:].rearrange("p (n j) -> p n j", j=4)
+            nc.scalar.activation(g4[:, :, 3], row3[:].indirect(offs_sb[:, cols]), ACT.Copy)
+
+            codes = keep.tile([P, n], U32, name=f"codes{c}", align_bytes=64)
+            x_scales = keep.tile([P, n], U8, name=f"x_scales{c}", align_bytes=64)
+            nc.vector.quantize_mx(out=codes[:].bitcast(FP8X4), scales=x_scales[:], in_=picked[c][:])
+
+            pre_gate = psum.tile([P, n], F32, name=f"pre_gate{c}")
+            pre_cand = psum.tile([P, n], F32, name=f"pre_cand{c}")
+            for acc, i in ((pre_gate, 1), (pre_cand, 0)):
+                nc.tensor.matmul_mx(
+                    out=acc[:], lhsT=words[i][:].bitcast(FP4X4), lhsT_scale=scales[i][:],
+                    rhs=codes[:].bitcast(FP8X4), rhs_scale=x_scales[:], start=True, stop=True,
+                )
+            gate = keep.tile([P, n], F32, name=f"gate{c}")
+            nc.scalar.activation(gate[:], pre_gate[:], ACT.Sigmoid)
+            gates.append(gate)
+            cands.append(pre_cand)
+            nc.vector.tensor_copy(old[:, a:b], memory[:].indirect(slot_sb[:, cols]))
+
+        for c, (a, b) in enumerate(spans(CHUNKS)):
+            gap = keep.tile([P, b - a], F32, name=f"gap{c}")
+            nc.vector.scalar_tensor_tensor(gap[:], cands[c][:], 0.0, old[:, a:b], ALU.max, ALU.subtract)
+            nc.vector.tensor_tensor(step[:, a:b], gap[:], gates[c][:], ALU.mult)
+        for c, (a, b) in enumerate(spans(CHUNKS)):
+            nc.vector.tensor_tensor(memory[:].indirect(slot_sb[:, a // 16 : b // 16]), old[:, a:b], step[:, a:b], ALU.add)
+
+        half = T // 2
+        nc.sync.dma_start(out[:, :half], memory[:, :half])
+        nc.scalar.dma_start(out[:, half:], memory[:, half:])

@@ -17,10 +17,11 @@ ACT = mybir.ActivationFunctionType
 ALU = mybir.AluOpType
 
 P = 128
-PAIR_COLS = [640,640,512,256]
+PAIR_COLS = [1024,640,384]
 ROW2_COLS = [1024,1024]
-ROW3_COLS = [1024,768,256]
-CHUNKS = [512,512]
+ROW3_COLS = [384,640,640,384]
+CHUNKS = [256,256,256,256]
+EARLY = 1
 
 
 def spans(widths):
@@ -37,38 +38,45 @@ def tile_picked_gmem_relu_e_kernel(tc, xT, mem, w1_words, w1_scales, w2_words, w
 
         offs_sb = keep.tile([P, S // 16], U16, name="offs_sb")
         slot_sb = keep.tile([P, S // 16], U16, name="slot_sb")
+        memory_in = keep.tile([P, T], F32, name="memory_in", tag="shared", align_bytes=64)
         memory = keep.tile([P, T], F32, name="memory")
         pairs = keep.tile([P, T], U32, name="pairs")
         row2 = keep.tile([P, T], BF16, name="row2")
         row3 = keep.tile([P, T], BF16, name="row3")
         old = keep.tile([P, S], F32, name="old")
         step = keep.tile([P, S], F32, name="step")
+        words = [keep.tile([P, 2 * N], U8, name=f"w_words{i}", align_bytes=64) for i in range(2)]
+        scales = [keep.tile([P, N], U8, name=f"w_scales{i}", align_bytes=64) for i in range(2)]
 
         warm_in = keep.tile([P, 1], F32, name="warm_in")
         warm_out = keep.tile([P, 1], F32, name="warm_out")
         nc.vector.memset(warm_in[:], 0.0)
         nc.scalar.activation(warm_out[:], warm_in[:], ACT.Sigmoid)
 
-        words = []
-        scales = []
-        for i, w_scales in enumerate((w1_scales, w2_scales)):
-            ws = keep.tile([P, N], U8, name=f"w_scales{i}", align_bytes=64)
-            nc.vector.memset(ws[:].bitcast(I32), 0)
-            for q in range(4):
-                nc.gpsimd.dma_start(ws[32 * q : 32 * q + 4, :].bitcast(I32), w_scales[0, 4 * q : 4 * q + 4, :].bitcast(I32))
-            scales.append(ws)
+        def load_scale_rows(i, q):
+            src = (w1_scales, w2_scales)[i]
+            nc.sync.dma_start(scales[i][32 * q : 32 * q + 4, :].bitcast(I32), src[0, 4 * q : 4 * q + 4, :].bitcast(I32))
 
-        for i, (a, b) in enumerate(spans(ROW2_COLS)):
-            raw = keep.tile([P, b - a], F32, name=f"raw_row2_{i}")
-            nc.sync.dma_start(raw[:], x_rows[:, 2, a:b])
-            nc.scalar.activation(row2[:, a:b], raw[:], ACT.Copy)
-        nc.sync.dma_start(offs_sb[:], offs)
+        def load_row(dst, j, a, b):
+            raw = keep.tile([P, b - a], F32, name=f"raw_row{j}_{a}")
+            nc.sync.dma_start(raw[:], x_rows[:, j, a:b])
+            nc.scalar.activation(dst[:, a:b], raw[:], ACT.Copy)
 
-        pairs_bf = pairs[:].bitcast(BF16).rearrange("p (t u) -> p t u", u=2)
-        for i, (a, b) in enumerate(spans(PAIR_COLS)):
-            raw = keep.tile([P, 2, b - a], F32, name=f"raw_pair{i}")
+        def load_pair(a, b):
+            raw = keep.tile([P, 2, b - a], F32, name=f"raw_pair{a}")
             nc.sync.dma_start(raw[:], x_rows[:, 0:2, a:b])
+            pairs_bf = pairs[:].bitcast(BF16).rearrange("p (t u) -> p t u", u=2)
             nc.vector.tensor_copy(pairs_bf[:, a:b, :], raw[:].rearrange("p u t -> p t u"))
+
+        for a, b in spans(ROW2_COLS):
+            load_row(row2, 2, a, b)
+        nc.sync.dma_start(offs_sb[:], offs)
+        pair_spans = spans(PAIR_COLS)
+        load_pair(*pair_spans[0])
+        for q in range(4):
+            load_scale_rows(0, q)
+        load_pair(*pair_spans[1])
+        load_pair(*pair_spans[2])
 
         picked = []
         for c, (a, b) in enumerate(spans(CHUNKS)):
@@ -80,48 +88,64 @@ def tile_picked_gmem_relu_e_kernel(tc, xT, mem, w1_words, w1_scales, w2_words, w
             g_words = picked[c][:].bitcast(U32).rearrange("p (n u) -> p n u", u=2)
             nc.vector.tensor_copy(g_words[:, :, 0], pairs[:].indirect(offs_sb[:, a // 16 : b // 16]))
 
-        for i, (a, b) in enumerate(spans(ROW3_COLS)):
-            raw = keep.tile([P, b - a], F32, name=f"raw_row3_{i}")
-            nc.sync.dma_start(raw[:], x_rows[:, 3, a:b])
-            nc.scalar.activation(row3[:, a:b], raw[:], ACT.Copy)
-        for i, w_words in enumerate((w1_words, w2_words)):
-            ww = keep.tile([P, 2 * N], U8, name=f"w_words{i}", align_bytes=64)
-            nc.sync.dma_start(ww[:], w_words[0])
-            words.append(ww)
+        row3_spans = spans(ROW3_COLS)
+        load_row(row3, 3, *row3_spans[0])
+        for q in range(4):
+            load_scale_rows(1, q)
+        for a, b in row3_spans[1:]:
+            load_row(row3, 3, a, b)
+        nc.sync.dma_start(words[0][:], w1_words[0])
+        nc.sync.dma_start(words[1][:], w2_words[0])
+        nc.sync.dma_start(memory_in[:], mem)
         nc.sync.dma_start(slot_sb[:], slot)
         nc.sync.dma_start(memory[:], mem)
 
+        for c, (a, b) in enumerate(spans(CHUNKS)):
+            g4 = picked[c][:].rearrange("p (n j) -> p n j", j=4)
+            nc.scalar.activation(g4[:, :, 3], row3[:].indirect(offs_sb[:, a // 16 : b // 16]), ACT.Copy)
+
         gates = []
         cands = []
-        for c, (a, b) in enumerate(spans(CHUNKS)):
+
+        def products(c, a, b, codes):
             n = b - a
-            cols = slice(a // 16, b // 16)
-            g4 = picked[c][:].rearrange("p (n j) -> p n j", j=4)
-            nc.scalar.activation(g4[:, :, 3], row3[:].indirect(offs_sb[:, cols]), ACT.Copy)
-
-            codes = keep.tile([P, n], U32, name=f"codes{c}", align_bytes=64)
             x_scales = keep.tile([P, n], U8, name=f"x_scales{c}", align_bytes=64)
-            nc.vector.quantize_mx(out=codes[:].bitcast(FP8X4), scales=x_scales[:], in_=picked[c][:])
-
+            nc.vector.quantize_mx(out=codes.bitcast(FP8X4), scales=x_scales[:], in_=picked[c][:])
             pre_gate = psum.tile([P, n], F32, name=f"pre_gate{c}")
             pre_cand = psum.tile([P, n], F32, name=f"pre_cand{c}")
-            for acc, i in ((pre_gate, 1), (pre_cand, 0)):
+            for acc, i in ((pre_cand, 0), (pre_gate, 1)):
                 nc.tensor.matmul_mx(
                     out=acc[:], lhsT=words[i][:].bitcast(FP4X4), lhsT_scale=scales[i][:],
-                    rhs=codes[:].bitcast(FP8X4), rhs_scale=x_scales[:], start=True, stop=True,
+                    rhs=codes.bitcast(FP8X4), rhs_scale=x_scales[:], start=True, stop=True,
                 )
             gate = keep.tile([P, n], F32, name=f"gate{c}")
             nc.scalar.activation(gate[:], pre_gate[:], ACT.Sigmoid)
             gates.append(gate)
             cands.append(pre_cand)
-            nc.vector.tensor_copy(old[:, a:b], memory[:].indirect(slot_sb[:, cols]))
 
-        for c, (a, b) in enumerate(spans(CHUNKS)):
+        chunks = spans(CHUNKS)
+        for c, (a, b) in enumerate(chunks[:EARLY]):
+            codes = keep.tile([P, b - a], U32, name=f"codes{c}", align_bytes=64)
+            products(c, a, b, codes[:])
+        nc.vector.tensor_copy(old[:], memory_in[:].indirect(slot_sb[:]))
+        first_late = chunks[EARLY][0]
+        late_codes = keep.tile([P, S - first_late], U32, name="late_codes", tag="shared", align_bytes=64)
+        for c, (a, b) in enumerate(chunks):
+            if c >= EARLY:
+                products(c, a, b, late_codes[:, a - first_late : b - first_late])
+
+        gaps = []
+        for c, (a, b) in enumerate(chunks):
             gap = keep.tile([P, b - a], F32, name=f"gap{c}")
             nc.vector.scalar_tensor_tensor(gap[:], cands[c][:], 0.0, old[:, a:b], ALU.max, ALU.subtract)
-            nc.vector.tensor_tensor(step[:, a:b], gap[:], gates[c][:], ALU.mult)
-        for c, (a, b) in enumerate(spans(CHUNKS)):
-            nc.vector.tensor_tensor(memory[:].indirect(slot_sb[:, a // 16 : b // 16]), old[:, a:b], step[:, a:b], ALU.add)
+            gaps.append(gap)
+            if c > 0:
+                pa, pb = chunks[c - 1]
+                nc.vector.tensor_tensor(step[:, pa:pb], gaps[c - 1][:], gates[c - 1][:], ALU.mult)
+        pa, pb = chunks[-1]
+        nc.vector.tensor_tensor(step[:, pa:pb], gaps[-1][:], gates[-1][:], ALU.mult)
+
+        nc.vector.tensor_tensor(memory[:].indirect(slot_sb[:]), old[:], step[:], ALU.add)
 
         half = T // 2
         nc.sync.dma_start(out[:, :half], memory[:, :half])

from contextlib import ExitStack

import concourse.mybir as mybir

K, T, S, N = 512, 2048, 1024, 128
FLOPS = 2 * 2 * K * S * N

F32 = mybir.dt.float32
BF16 = mybir.dt.bfloat16
I32 = mybir.dt.int32
U32 = mybir.dt.uint32
U16 = mybir.dt.uint16
U8 = mybir.dt.uint8
FP8X4 = mybir.dt.float8_e4m3fn_x4
FP4X4 = mybir.dt.float4_e2m1fn_x4
ACT = mybir.ActivationFunctionType
ALU = mybir.AluOpType

P = 128
PAIR_COLS = [1024,640,384]
ROW2_COLS = [1024,1024]
ROW3_COLS = [384,640,640,384]
CHUNKS = [256,256,256,256]
EARLY = 1


def spans(widths):
    return [(sum(widths[:i]), sum(widths[: i + 1])) for i in range(len(widths))]


def tile_picked_gmem_relu_e_kernel(tc, xT, mem, w1_words, w1_scales, w2_words, w2_scales, offs, slot, out):
    nc = tc.nc
    x_rows = xT.rearrange("(p j) t -> p j t", j=4)

    with ExitStack() as ctx:
        keep = ctx.enter_context(tc.tile_pool(name="keep", bufs=1))
        psum = ctx.enter_context(tc.psum_pool(name="psum", bufs=1))

        offs_sb = keep.tile([P, S // 16], U16, name="offs_sb")
        slot_sb = keep.tile([P, S // 16], U16, name="slot_sb")
        memory_in = keep.tile([P, T], F32, name="memory_in", tag="shared", align_bytes=64)
        memory = keep.tile([P, T], F32, name="memory")
        pairs = keep.tile([P, T], U32, name="pairs")
        row2 = keep.tile([P, T], BF16, name="row2")
        row3 = keep.tile([P, T], BF16, name="row3")
        old = keep.tile([P, S], F32, name="old")
        step = keep.tile([P, S], F32, name="step")
        words = [keep.tile([P, 2 * N], U8, name=f"w_words{i}", align_bytes=64) for i in range(2)]
        scales = [keep.tile([P, N], U8, name=f"w_scales{i}", align_bytes=64) for i in range(2)]

        warm_in = keep.tile([P, 1], F32, name="warm_in")
        warm_out = keep.tile([P, 1], F32, name="warm_out")
        nc.vector.memset(warm_in[:], 0.0)
        nc.scalar.activation(warm_out[:], warm_in[:], ACT.Sigmoid)

        def load_scale_rows(i, q):
            src = (w1_scales, w2_scales)[i]
            nc.sync.dma_start(scales[i][32 * q : 32 * q + 4, :].bitcast(I32), src[0, 4 * q : 4 * q + 4, :].bitcast(I32))

        def load_row(dst, j, a, b):
            raw = keep.tile([P, b - a], F32, name=f"raw_row{j}_{a}")
            nc.sync.dma_start(raw[:], x_rows[:, j, a:b])
            nc.scalar.activation(dst[:, a:b], raw[:], ACT.Copy)

        def load_pair(a, b):
            raw = keep.tile([P, 2, b - a], F32, name=f"raw_pair{a}")
            nc.sync.dma_start(raw[:], x_rows[:, 0:2, a:b])
            pairs_bf = pairs[:].bitcast(BF16).rearrange("p (t u) -> p t u", u=2)
            nc.vector.tensor_copy(pairs_bf[:, a:b, :], raw[:].rearrange("p u t -> p t u"))

        for a, b in spans(ROW2_COLS):
            load_row(row2, 2, a, b)
        nc.sync.dma_start(offs_sb[:], offs)
        pair_spans = spans(PAIR_COLS)
        load_pair(*pair_spans[0])
        for q in range(4):
            load_scale_rows(0, q)
        load_pair(*pair_spans[1])
        load_pair(*pair_spans[2])

        picked = []
        for c, (a, b) in enumerate(spans(CHUNKS)):
            g = keep.tile([P, 4 * (b - a)], BF16, name=f"picked{c}", align_bytes=64)
            picked.append(g)
            g4 = g[:].rearrange("p (n j) -> p n j", j=4)
            nc.scalar.activation(g4[:, :, 2], row2[:].indirect(offs_sb[:, a // 16 : b // 16]), ACT.Copy)
        for c, (a, b) in enumerate(spans(CHUNKS)):
            g_words = picked[c][:].bitcast(U32).rearrange("p (n u) -> p n u", u=2)
            nc.vector.tensor_copy(g_words[:, :, 0], pairs[:].indirect(offs_sb[:, a // 16 : b // 16]))

        row3_spans = spans(ROW3_COLS)
        load_row(row3, 3, *row3_spans[0])
        for q in range(4):
            load_scale_rows(1, q)
        for a, b in row3_spans[1:]:
            load_row(row3, 3, a, b)
        nc.sync.dma_start(words[0][:], w1_words[0])
        nc.sync.dma_start(words[1][:], w2_words[0])
        nc.sync.dma_start(memory_in[:], mem)
        nc.sync.dma_start(slot_sb[:], slot)
        nc.sync.dma_start(memory[:], mem)

        for c, (a, b) in enumerate(spans(CHUNKS)):
            g4 = picked[c][:].rearrange("p (n j) -> p n j", j=4)
            nc.scalar.activation(g4[:, :, 3], row3[:].indirect(offs_sb[:, a // 16 : b // 16]), ACT.Copy)

        gates = []
        cands = []

        def products(c, a, b, codes):
            n = b - a
            x_scales = keep.tile([P, n], U8, name=f"x_scales{c}", align_bytes=64)
            nc.vector.quantize_mx(out=codes.bitcast(FP8X4), scales=x_scales[:], in_=picked[c][:])
            pre_gate = psum.tile([P, n], F32, name=f"pre_gate{c}")
            pre_cand = psum.tile([P, n], F32, name=f"pre_cand{c}")
            for acc, i in ((pre_cand, 0), (pre_gate, 1)):
                nc.tensor.matmul_mx(
                    out=acc[:], lhsT=words[i][:].bitcast(FP4X4), lhsT_scale=scales[i][:],
                    rhs=codes.bitcast(FP8X4), rhs_scale=x_scales[:], start=True, stop=True,
                )
            gate = keep.tile([P, n], F32, name=f"gate{c}")
            nc.scalar.activation(gate[:], pre_gate[:], ACT.Sigmoid)
            gates.append(gate)
            cands.append(pre_cand)

        chunks = spans(CHUNKS)
        for c, (a, b) in enumerate(chunks[:EARLY]):
            codes = keep.tile([P, b - a], U32, name=f"codes{c}", align_bytes=64)
            products(c, a, b, codes[:])
        nc.vector.tensor_copy(old[:], memory_in[:].indirect(slot_sb[:]))
        first_late = chunks[EARLY][0]
        late_codes = keep.tile([P, S - first_late], U32, name="late_codes", tag="shared", align_bytes=64)
        for c, (a, b) in enumerate(chunks):
            if c >= EARLY:
                products(c, a, b, late_codes[:, a - first_late : b - first_late])

        gaps = []
        for c, (a, b) in enumerate(chunks):
            gap = keep.tile([P, b - a], F32, name=f"gap{c}")
            nc.vector.scalar_tensor_tensor(gap[:], cands[c][:], 0.0, old[:, a:b], ALU.max, ALU.subtract)
            gaps.append(gap)
            if c > 0:
                pa, pb = chunks[c - 1]
                nc.vector.tensor_tensor(step[:, pa:pb], gaps[c - 1][:], gates[c - 1][:], ALU.mult)
        pa, pb = chunks[-1]
        nc.vector.tensor_tensor(step[:, pa:pb], gaps[-1][:], gates[-1][:], ALU.mult)

        nc.vector.tensor_tensor(memory[:].indirect(slot_sb[:]), old[:], step[:], ALU.add)

        half = T // 2
        nc.sync.dma_start(out[:, :half], memory[:, :half])
        nc.scalar.dma_start(out[:, half:], memory[:, half:])
